import numpy as np
import ml_dtypes


def mxq(x, axis, fmt="e4m3"):
    dtype, down = {"e4m3": (ml_dtypes.float8_e4m3fn, 7), "e5m2": (ml_dtypes.float8_e5m2, 14)}[fmt]
    v = np.moveaxis(np.asarray(x, np.float32).astype(ml_dtypes.bfloat16).astype(np.float64), axis, -1)
    blocks = v.reshape(v.shape[:-1] + (-1, 32))
    amax = np.abs(blocks).max(-1, keepdims=True)
    byte = np.maximum(np.where(amax > 0, np.frexp(amax)[1] - 1 + 127, 0) - down, 1)
    scale = np.exp2(byte - 127.0)
    codes = (blocks / scale).astype(np.float32).astype(dtype).astype(np.float64)
    return np.moveaxis((codes * scale).reshape(v.shape), -1, axis)


WIDE = False


def mx_kscale(k):
    if not WIDE:
        return np.ones(k)
    levels = np.array([10, -10, 5, -5, 0])
    if k % 512:
        return np.exp2(np.random.permutation(np.resize(levels, k // 32))).repeat(32)
    a = np.empty((k // 512, 16))
    for p in range(k // 512):
        a[p, :8] = np.random.permutation(np.resize(levels, 8))
        for g in range(8):
            far = levels[np.abs(levels - a[p, g]) >= 10]
            a[p, g + 8] = far[np.random.randint(len(far))]
    return np.exp2(a.ravel()).repeat(32)


def f64(x):
    return np.asarray(x).astype(np.float64)


def striped(idx):
    return np.tile(idx.reshape(-1, 16).T, (8, 1)).astype(np.uint16)


def unstriped(offs):
    return offs[:16].T.reshape(-1).astype(np.int64)


E2M1 = np.array([0.0, 0.5, 1.0, 1.5, 2.0, 3.0, 4.0, 6.0, -0.0, -0.5, -1.0, -1.5, -2.0, -3.0, -4.0, -6.0])


def pack_weight(w, fmt):
    k, n = w.shape
    w = f64(np.asarray(w, np.float32).astype(ml_dtypes.bfloat16)).reshape(k // 32, 32, n)
    amax = np.abs(w).max(1)
    if fmt == "e4m3":
        byte = np.frexp(amax)[1] - 1 + 127 - 7
    else:
        mant, ex = np.frexp(amax / 6.0)
        byte = np.where(mant > 0.5, ex, ex - 1) + 127
    byte = np.clip(np.where(amax > 0, byte, 1), 1, 254)
    scaled = (w * np.exp2(127.0 - byte)[:, None, :]).reshape(k, n).astype(np.float32)
    by_word = np.ascontiguousarray(scaled.reshape(k // 512, 128, 4, n).transpose(0, 1, 3, 2))
    if fmt == "e4m3":
        words = by_word.astype(ml_dtypes.float8_e4m3fn).view(np.uint8)
    else:
        c = by_word.astype(ml_dtypes.float4_e2m1fn).view(np.uint8) & 0xF
        words = (c[..., 0::2] | (c[..., 1::2] << 4)).reshape(k // 512, 128, 2 * n)
    return np.ascontiguousarray(words), np.ascontiguousarray(byte.astype(np.uint8).reshape(k // 512, 16, n))


def unpack_weight(words, scales, fmt):
    g, _, n = scales.shape
    words = np.ascontiguousarray(words).reshape(g, 128, n, -1)
    if fmt == "e4m3":
        vals = words.view(ml_dtypes.float8_e4m3fn).astype(np.float64)
    else:
        nib = np.empty((g, 128, n, 4), np.uint8)
        nib[..., 0::2] = words & 0xF
        nib[..., 1::2] = words >> 4
        vals = E2M1[nib]
    vals = vals * np.repeat(np.exp2(scales.astype(np.float64) - 127.0), 8, axis=1)[..., None]
    return vals.transpose(0, 1, 3, 2).reshape(g * 512, n)


K, T, E, C, N = 512, 1024, 16, 256, 256
TOP = 4


def by_expert(wq, xq):
    return np.concatenate([wq[e].T @ xq[:, e * C:(e + 1) * C] for e in range(E)], axis=1)


def setup_inputs():
    n = np.random.standard_normal
    s = mx_kscale(K)[:, None]
    deal = np.repeat(np.arange(E), C).reshape(TOP, T)[:, np.random.permutation(T)]
    deal = np.take_along_axis(deal, np.argsort(np.random.rand(TOP, T), axis=0), axis=0)
    for _ in range(8):
        s_, t_ = np.random.permutation(T).reshape(2, -1); r = np.random.randint(TOP, size=T // 2); x, y = deal[r, s_].copy(), deal[r, t_].copy()
        ok = ~((deal[:, s_] == y).any(0) | (deal[:, t_] == x).any(0)); deal[r[ok], s_[ok]] = y[ok]; deal[r[ok], t_[ok]] = x[ok]
    order = np.lexsort((np.random.rand(TOP * T), deal.reshape(-1)))
    slot_token = order % T; pos = np.empty(TOP * T, np.int64); pos[order] = np.arange(TOP * T); pos = pos.reshape(TOP, T)
    g = np.random.uniform(0.5, 1.5, (TOP, T)); g = g / g.sum(0)
    x = pack_weight(n((K, T)) * s, "e4m3")
    return {
        "x_words": x[0],
        "x_scales": x[1],
        "w": (n((E + 1, K, N)) / np.sqrt(K) / s[None]).astype(np.float32),
        "gate": np.stack([np.tile(r, (N, 1)) for r in g]).astype(np.float32),
        "offs": striped(slot_token),
        "pos1": striped(pos[0]),
        "pos2": striped(pos[1]),
        "pos3": striped(pos[2]),
        "pos4": striped(pos[3]),
    }


def reference(x_words, x_scales, w, gate, offs, pos1, pos2, pos3, pos4):
    idx = unstriped(offs)
    wq = mxq(f64(w), 1, "e4m3")
    xs = unpack_weight(x_words, x_scales, "e4m3")
    ys = wq[E].T @ xs
    xq = unpack_weight(x_words, x_scales, "e4m3")[:, idx]
    y = by_expert(wq, xq)
    return ys + sum(f64(gate[r]) * y[:, unstriped(p)] for r, p in enumerate((pos1, pos2, pos3, pos4)))

@@ -1,0 +1,270 @@
+from contextlib import ExitStack
+
+import concourse.mybir as mybir
+from concourse.masks import make_identity
+
+K, T, E, C, N = 512, 1024, 16, 256, 256
+TOP = 4
+SLOTS = E * C
+FLOPS = 2 * K * N * (SLOTS + T)
+
+F32 = mybir.dt.float32
+BF16 = mybir.dt.bfloat16
+I32 = mybir.dt.int32
+U32 = mybir.dt.uint32
+U16 = mybir.dt.uint16
+U8 = mybir.dt.uint8
+FP8X4 = mybir.dt.float8_e4m3fn_x4
+MULT = mybir.AluOpType.mult
+ADD = mybir.AluOpType.add
+
+P = 128
+PACK = 4
+BANK = 512
+PER_COL = 16
+GATHER = 768
+
+
+def tile_moe_shr_lin_none_kernel(
+    tc, x_words, x_scales, w, gate, offs, pos1, pos2, pos3, pos4, out
+):
+    nc = tc.nc
+    with ExitStack() as ctx:
+        keep = ctx.enter_context(tc.tile_pool(name="keep", bufs=1))
+        shared = ctx.enter_context(tc.tile_pool(name="shared", bufs=1))
+        ring = ctx.enter_context(tc.tile_pool(name="ring", bufs=2))
+        psum = ctx.enter_context(tc.psum_pool(name="psum", bufs=1))
+
+        offs_sb = keep.tile([P, SLOTS // PER_COL], U16, name="offs_sb")
+        pos_sb = [keep.tile([P, T // PER_COL], U16, name="pos_sb%d" % r) for r in range(TOP)]
+        tok_words = keep.tile([P, T], I32, name="tok_words", align_bytes=64)
+        tok_scales = keep.tile([P, T], U8, name="tok_scales", align_bytes=64)
+        widths = [min(GATHER, SLOTS - a) for a in range(0, SLOTS, GATHER)]
+        slot_words = [keep.tile([P, n], U32, name="slot_words%d" % i, align_bytes=64)[:] for i, n in enumerate(widths)]
+        slot_scales = [keep.tile([P, GATHER], U8, name="slot_scales%d" % i, align_bytes=64)[:] for i in range(3)]
+        y = [keep.tile([P, SLOTS], F32, name="y%d" % h) for h in range(2)]
+        ys = [keep.tile([P, T], F32, name="ys%d" % h) for h in range(2)]
+        ident = keep.tile([P, P], F32, name="ident")
+
+        nc.sync.dma_start(offs_sb[:], offs)
+        nc.sync.dma_start(tok_words[:], x_words[0].rearrange("p t r -> p (t r)").bitcast(I32))
+        nc.gpsimd.memset(tok_scales[:].bitcast(I32), 0)
+        for q in range(4):
+            nc.sync.dma_start(
+                tok_scales[32 * q : 32 * q + 4, :].bitcast(I32), x_scales[0, 4 * q : 4 * q + 4, :].bitcast(I32)
+            )
+        make_identity(nc, ident[:])
+
+        def on_bytes_of_w(e, shape, dtype, name):
+            return shared.tile(shape, dtype, name=name, tag="w%d" % e, align_bytes=64)
+
+        def load_w(e):
+            rows = w[e].rearrange("(p j) n -> p j n", j=PACK)
+            if e != E - 1:
+                raw = on_bytes_of_w(e, [P, PACK, N], F32, "w_raw%d" % e)
+                nc.sync.dma_start(raw[:], rows)
+                return [raw[:, :, :P], raw[:, :, P:], raw[:]]
+            halves = [on_bytes_of_w(e, [P, PACK, P], F32, "w_last0"), keep.tile([P, PACK, P], F32, name="w_last1")]
+            for h in range(2):
+                nc.sync.dma_start(halves[h][:], rows[:, :, h * P : (h + 1) * P])
+            return [half[:] for half in halves]
+
+        def load_gate(r, h, g):
+            nc.sync.dma_start(g[:], gate[r, h * P : (h + 1) * P, :])
+            return g
+
+        w_raw = [load_w(e) for e in range(E)]
+        gates = {}
+        for r, pos in enumerate((pos1, pos2, pos3, pos4)):
+            nc.sync.dma_start(pos_sb[r][:], pos)
+            gates[r, 0] = load_gate(r, 0, keep.tile([P, T], F32, name="gate%d_0" % r))
+            if r == 0:
+                w_raw.append(load_w(E))
+
+        def gather(dst, window, i):
+            a, b = i * GATHER, min((i + 1) * GATHER, SLOTS)
+            nc.vector.tensor_copy(dst[i], window.indirect(offs_sb[:, a // PER_COL : b // PER_COL]))
+
+        def gather_words(i):
+            gather(slot_words, tok_words[:].bitcast(U32), i)
+
+        def gather_scales(i):
+            gather(slot_scales, tok_scales[:], i)
+
+        def interleave(dst, e, h):
+            nc.scalar.copy(
+                dst.rearrange("p (c i) j -> p c j i", i=4),
+                w_raw[e][h].rearrange("p j (c i) -> p c j i", i=4),
+            )
+
+        def interleave_both(dst, e):
+            nc.scalar.copy(
+                dst.rearrange("p h (c i) j -> p h c j i", i=4),
+                w_raw[e][2].rearrange("p j (h c i) -> p h c j i", h=2, i=4),
+            )
+
+        def quantize(codes, scales, rounded):
+            nc.vector.quantize_mx(
+                out=codes.bitcast(FP8X4), scales=scales, in_=rounded.rearrange("p s n j -> p (s n j)")
+            )
+
+        def mx(dst, codes, scales, s, words, word_scales):
+            nc.tensor.matmul_mx(
+                out=dst,
+                lhsT=codes[:, s * P : (s + 1) * P].bitcast(FP8X4),
+                lhsT_scale=scales[:, s * P : (s + 1) * P],
+                rhs=words.bitcast(FP8X4),
+                rhs_scale=word_scales,
+                start=True,
+                stop=True,
+            )
+
+        for i in range(len(widths)):
+            gather_words(i)
+            if i in (1, 3, 5):
+                gather_scales(i // 2)
+
+        w_bf = keep.tile([P, 2, E, P, PACK], BF16, name="w_bf", align_bytes=64)
+        early = 12
+        for e in range(early):
+            interleave_both(w_bf[:, :, e, :, :], e)
+        for e in range(early, E):
+            interleave(w_bf[:, 0, e, :, :], e, 0)
+        for r in range(TOP):
+            gates[r, 1] = load_gate(r, 1, on_bytes_of_w(r, [P, T], F32, "gate%d_1" % r))
+
+        w_codes = [on_bytes_of_w(e, [P, E * P], U32, "w_codes%d" % h) for h, e in enumerate((9, E - 1))]
+        w_scales = [keep.tile([P, E * P], U8, name="w_scales%d" % h, align_bytes=64) for h in range(2)]
+
+        def quantize_experts(h, first, count):
+            cols = slice(first * P, (first + count) * P)
+            quantize(w_codes[h][:, cols], w_scales[h][:, cols], w_bf[:, h, first : first + count, :, :])
+
+        def multiply_experts(h, first, count):
+            for e0 in range(first, first + count, 2):
+                bank = psum.tile([P, BANK], F32, name="y_bank", tag="y_bank", bufs=3)
+                for e in (e0, e0 + 1):
+                    i, a = divmod(e * C, GATHER)
+                    mx(
+                        bank[:, (e - e0) * C : (e - e0 + 1) * C],
+                        w_codes[h],
+                        w_scales[h],
+                        e,
+                        slot_words[i][:, a : a + C],
+                        slot_scales[i][:, a : a + C],
+                    )
+                nc.scalar.copy(y[h][:, e0 * C : (e0 + 2) * C], bank[:])
+
+        quantize_experts(0, 0, 4)
+        quantize_experts(0, 4, 4)
+        multiply_experts(0, 0, 8)
+        slot_scales.append(on_bytes_of_w(10, [P, GATHER], U8, "slot_scales3")[:])
+        gather_scales(3)
+        quantize_experts(0, 8, 4)
+        multiply_experts(0, 8, 4)
+        last_scales = on_bytes_of_w(11, [P, SLOTS - 4 * GATHER], U8, "slot_scales4")
+        slot_scales.extend([last_scales[:, :GATHER], last_scales[:, GATHER:]])
+        gather_scales(4)
+        gather_scales(5)
+        quantize_experts(0, 12, 2)
+        quantize_experts(0, 14, 2)
+        multiply_experts(0, 12, 4)
+
+        ws_bf = keep.tile([P, 2, P, PACK], BF16, name="ws_bf", align_bytes=64)
+        ws_codes = keep.tile([P, N], U32, name="ws_codes", align_bytes=64)
+        ws_scales = keep.tile([P, N], U8, name="ws_scales", align_bytes=64)
+        interleave_both(ws_bf[:], E)
+        for e in range(early, E):
+            interleave(w_bf[:, 1, e, :, :], e, 1)
+        for first in range(0, E, 4):
+            quantize_experts(1, first, 4)
+        quantize(ws_codes[:], ws_scales[:], ws_bf[:])
+
+        def multiply_shared(h):
+            for t0 in range(0, T, BANK):
+                bank = psum.tile([P, BANK], F32, name="y_bank", tag="y_bank", bufs=3)
+                mx(bank[:], ws_codes, ws_scales, h, tok_words[:, t0 : t0 + BANK], tok_scales[:, t0 : t0 + BANK])
+                nc.scalar.copy(ys[h][:, t0 : t0 + BANK], bank[:])
+
+        multiply_experts(1, 0, early)
+        multiply_shared(0)
+        multiply_experts(1, early, E - early)
+
+        def product(dst, h, r, t0):
+            width = dst.shape[1]
+            nc.vector.tensor_tensor(
+                dst,
+                y[h][:].indirect(pos_sb[r][:, t0 // PER_COL : (t0 + width) // PER_COL]),
+                gates[r, h][:, t0 : t0 + width],
+                MULT,
+            )
+            return dst
+
+        def turn(terms, turned_sb):
+            width = turned_sb.shape[1]
+            blocks = width // P
+            turned = psum.tile([P, BANK], F32, name="turned", tag="turned", bufs=3)
+            for i, term in enumerate(terms):
+                for b in range(blocks):
+                    nc.tensor.matmul(
+                        turned[:, b * P : (b + 1) * P],
+                        term[:, b * P : (b + 1) * P],
+                        ident[:],
+                        start=(i == 0 and b == 0),
+                        stop=(i == len(terms) - 1 and b == blocks - 1),
+                        is_transpose=True,
+                    )
+            nc.scalar.copy(turned_sb, turned[:, :width])
+
+        def turn_back(turned_sb):
+            back = psum.tile([P, BANK], F32, name="back", tag="back", bufs=2)
+            for b in range(turned_sb.shape[1] // P):
+                nc.tensor.transpose(back[:, b * P : (b + 1) * P], turned_sb[:, b * P : (b + 1) * P], ident[:])
+            return back
+
+        def store(res, h, t0):
+            nc.sync.dma_start(out[h * P : (h + 1) * P, t0 : t0 + res.shape[1]], res)
+
+        def finish(turned_sb, h, t0):
+            back = turn_back(turned_sb)
+            res = ring.tile([P, BANK], F32, name="res", tag="res", bufs=3)
+            nc.scalar.copy(res[:], back[:])
+            store(res[:], h, t0)
+
+        def lane(i, name):
+            return shared.tile([P, BANK], F32, name=name, tag="lane%d" % i)[:]
+
+        sums = []
+        for c in range(2):
+            pairs = [on_bytes_of_w(4 + 2 * c + i, [P, 2, BANK], F32, "prod%d_%d" % (c, i)) for i in range(2)]
+            prods = [product(pairs[r // 2][:, r % 2, :], 0, r, c * BANK) for r in range(TOP)]
+            sums.append(lane(c, "sum0_%d" % c))
+            turn(prods + [ys[0][:, c * BANK : (c + 1) * BANK]], sums[c])
+        multiply_shared(1)
+        for c in range(2):
+            finish(sums[c], 0, c * BANK)
+
+        pair = on_bytes_of_w(8, [P, 2, BANK], F32, "prod2")
+        prods = [product(pair[:, r, :], 1, r, 0) for r in range(2)]
+        prods += [product(lane(r % 2, "prod2_%d" % r), 1, r, 0) for r in (2, 3)]
+        turned_sb = ring.tile([P, BANK], F32, name="turned_sb", tag="turned_sb", bufs=3)
+        turn(prods[:2] + [ys[1][:, :BANK]] + prods[2:], turned_sb[:])
+        finish(turned_sb[:], 1, 0)
+
+        half = BANK // 2
+        wide = [product(lane(r, "prod3_%d" % r), 1, r, BANK) for r in range(2)]
+        third = lane(0, "prod3_2")
+        backs = []
+        for a in (0, half):
+            product(third[:, a : a + half], 1, 2, BANK + a)
+            terms = [ys[1][:, BANK + a : BANK + a + half]] + [g[:, a : a + half] for g in wide + [third]]
+            turned_sb = ring.tile([P, BANK], F32, name="turned_sb", tag="turned_sb", bufs=3)
+            turn(terms, turned_sb[:, :half])
+            backs.append(turn_back(turned_sb[:, :half]))
+        last = lane(1, "prod3_3")
+        for a in (0, half):
+            product(last[:, a : a + half], 1, 3, BANK + a)
+        for a, back in zip((0, half), backs):
+            res = ring.tile([P, BANK], F32, name="res", tag="res", bufs=3)
+            nc.vector.tensor_tensor(res[:, :half], back[:, :half], last[:, a : a + half], ADD)
+            store(res[:, :half], 1, BANK + a)

@@ -126,7 +126,12 @@ def tile_moe_shr_lin_none_kernel(
 
         w_bf = keep.tile([P, 2, E, P, PACK], BF16, name="w_bf", align_bytes=64)
         early = 12
-        for e in range(early):
+        for e in range(early - 2):
+            interleave(w_bf[:, 0, e, :, :], e, 0)
+            nc.gpsimd.tensor_scalar(
+                w_bf[:, 1, e, :, :], w_raw[e][1].rearrange("p j n -> p n j"), 1.0, 0.0, MULT, ADD
+            )
+        for e in range(early - 2, early):
             interleave_both(w_bf[:, :, e, :, :], e)
         for e in range(early, E):
             interleave(w_bf[:, 0, e, :, :], e, 0)

@@ -22,7 +22,8 @@ P = 128
 PACK = 4
 BANK = 512
 PER_COL = 16
-GATHER = 768
+GATHER = 1536
+WINDOW = 2048
 
 
 def tile_moe_shr_lin_none_kernel(
@@ -37,21 +38,19 @@ def tile_moe_shr_lin_none_kernel(
 
         offs_sb = keep.tile([P, SLOTS // PER_COL], U16, name="offs_sb")
         pos_sb = [keep.tile([P, T // PER_COL], U16, name="pos_sb%d" % r) for r in range(TOP)]
-        tok_words = keep.tile([P, T], I32, name="tok_words", align_bytes=64)
-        tok_scales = keep.tile([P, T], U8, name="tok_scales", align_bytes=64)
-        widths = [min(GATHER, SLOTS - a) for a in range(0, SLOTS, GATHER)]
-        slot_words = [keep.tile([P, n], U32, name="slot_words%d" % i, align_bytes=64)[:] for i, n in enumerate(widths)]
-        slot_scales = [keep.tile([P, GATHER], U8, name="slot_scales%d" % i, align_bytes=64)[:] for i in range(3)]
+        tok_words = keep.tile([P, WINDOW], I32, name="tok_words", align_bytes=64)
+        tok_scales = keep.tile([P, WINDOW], U8, name="tok_scales", align_bytes=64)
         y = [keep.tile([P, SLOTS], F32, name="y%d" % h) for h in range(2)]
         ys = [keep.tile([P, T], F32, name="ys%d" % h) for h in range(2)]
         ident = keep.tile([P, P], F32, name="ident")
 
         nc.sync.dma_start(offs_sb[:], offs)
-        nc.sync.dma_start(tok_words[:], x_words[0].rearrange("p t r -> p (t r)").bitcast(I32))
+        nc.sync.dma_start(tok_words[:, :T], x_words[0].rearrange("p t r -> p (t r)").bitcast(I32))
         nc.gpsimd.memset(tok_scales[:].bitcast(I32), 0)
+        nc.gpsimd.memset(tok_words[:, T:], 0)
         for q in range(4):
             nc.sync.dma_start(
-                tok_scales[32 * q : 32 * q + 4, :].bitcast(I32), x_scales[0, 4 * q : 4 * q + 4, :].bitcast(I32)
+                tok_scales[32 * q : 32 * q + 4, :T].bitcast(I32), x_scales[0, 4 * q : 4 * q + 4, :].bitcast(I32)
             )
         make_identity(nc, ident[:])
 
@@ -70,26 +69,36 @@ def tile_moe_shr_lin_none_kernel(
             return [half[:] for half in halves]
 
         def load_gate(r, h, g):
-            nc.sync.dma_start(g[:], gate[r, h * P : (h + 1) * P, :])
+            nc.sync.dma_start(g, gate[r, h * P : (h + 1) * P, :])
             return g
 
-        w_raw = [load_w(e) for e in range(E)]
+        def load_w_pair(e):
+            raw = on_bytes_of_w(e, [P, 2, PACK, N], F32, "w_raw%d" % e)
+            nc.sync.dma_start(raw[:], w[e : e + 2].rearrange("e (p j) n -> p e j n", j=PACK))
+            return [[raw[:, i, :, :P], raw[:, i, :, P:]] for i in range(2)]
+
+        w_raw = [one for e in range(0, 8, 2) for one in load_w_pair(e)] + [load_w(e) for e in range(8, E)]
         gates = {}
         for r, pos in enumerate((pos1, pos2, pos3, pos4)):
             nc.sync.dma_start(pos_sb[r][:], pos)
-            gates[r, 0] = load_gate(r, 0, keep.tile([P, T], F32, name="gate%d_0" % r))
+            gates[r, 0] = load_gate(r, 0, keep.tile([P, T], F32, name="gate%d_0" % r)[:])
             if r == 0:
                 w_raw.append(load_w(E))
 
-        def gather(dst, window, i):
-            a, b = i * GATHER, min((i + 1) * GATHER, SLOTS)
-            nc.vector.tensor_copy(dst[i], window.indirect(offs_sb[:, a // PER_COL : b // PER_COL]))
+        slot_words, slot_scales = {}, {}
 
-        def gather_words(i):
-            gather(slot_words, tok_words[:].bitcast(U32), i)
+        def gather(by_expert, dst, window, first):
+            count = dst.shape[1] // C
+            cols = slice(first * C // PER_COL, (first + count) * C // PER_COL)
+            nc.vector.tensor_copy(dst[:], window.indirect(offs_sb[:, cols]))
+            for i in range(count):
+                by_expert[first + i] = dst[:, i * C : (i + 1) * C]
 
-        def gather_scales(i):
-            gather(slot_scales, tok_scales[:], i)
+        def gather_words(dst, first):
+            gather(slot_words, dst, tok_words[:].bitcast(U32), first)
+
+        def gather_scales(dst, first):
+            gather(slot_scales, dst, tok_scales[:], first)
 
         def interleave(dst, e, h):
             nc.scalar.copy(
@@ -119,81 +128,77 @@ def tile_moe_shr_lin_none_kernel(
                 stop=True,
             )
 
-        for i in range(len(widths)):
-            gather_words(i)
-            if i in (1, 3, 5):
-                gather_scales(i // 2)
+        for first in (0, 6):
+            gather_words(keep.tile([P, 6 * C], U32, name="slot_words%d" % first, align_bytes=64), first)
+        for first, count in ((0, 6), (6, 2)):
+            gather_scales(keep.tile([P, count * C], U8, name="slot_scales%d" % first, align_bytes=64), first)
 
-        w_bf = keep.tile([P, 2, E, P, PACK], BF16, name="w_bf", align_bytes=64)
-        early = 12
-        for e in range(early - 2):
-            interleave(w_bf[:, 0, e, :, :], e, 0)
+        w_bf = {
+            (0, 0): keep.tile([P, 8, P, PACK], BF16, name="w_bf00", align_bytes=64),
+            (0, 8): shared.tile([P, 8, P, PACK], BF16, name="w_bf08", tag="late", align_bytes=64),
+            (1, 0): keep.tile([P, 8, P, PACK], BF16, name="w_bf10", align_bytes=64),
+            (1, 8): keep.tile([P, 8, P, PACK], BF16, name="w_bf18", align_bytes=64),
+        }
+        for e in range(E):
+            interleave(w_bf[0, e // 8 * 8][:, e % 8, :, :], e, 0)
+        for e in range(E - 2):
             nc.gpsimd.tensor_scalar(
-                w_bf[:, 1, e, :, :], w_raw[e][1].rearrange("p j n -> p n j"), 1.0, 0.0, MULT, ADD
+                w_bf[1, e // 8 * 8][:, e % 8, :, :], w_raw[e][1].rearrange("p j n -> p n j"), 1.0, 0.0, MULT, ADD
             )
-        for e in range(early - 2, early):
-            interleave_both(w_bf[:, :, e, :, :], e)
-        for e in range(early, E):
-            interleave(w_bf[:, 0, e, :, :], e, 0)
-        for r in range(TOP):
-            gates[r, 1] = load_gate(r, 1, on_bytes_of_w(r, [P, T], F32, "gate%d_1" % r))
+        for r in range(0, TOP, 2):
+            pair = on_bytes_of_w(r, [P, 2, T], F32, "gate%d_1" % r)
+            for i in range(2):
+                gates[r + i, 1] = load_gate(r + i, 1, pair[:, i, :])
 
-        w_codes = [on_bytes_of_w(e, [P, E * P], U32, "w_codes%d" % h) for h, e in enumerate((9, E - 1))]
+        w_codes = [shared.tile([P, E * P], U32, name="w_codes0", tag="codes0", align_bytes=64)]
         w_scales = [keep.tile([P, E * P], U8, name="w_scales%d" % h, align_bytes=64) for h in range(2)]
 
-        def quantize_experts(h, first, count):
-            cols = slice(first * P, (first + count) * P)
-            quantize(w_codes[h][:, cols], w_scales[h][:, cols], w_bf[:, h, first : first + count, :, :])
+        def quantize_experts(h, first):
+            cols = slice(first * P, (first + 8) * P)
+            quantize(w_codes[h][:, cols], w_scales[h][:, cols], w_bf[h, first][:])
 
         def multiply_experts(h, first, count):
             for e0 in range(first, first + count, 2):
-                bank = psum.tile([P, BANK], F32, name="y_bank", tag="y_bank", bufs=3)
+                bank = psum.tile([P, BANK], F32, name="y_bank", tag="bank", bufs=4)
                 for e in (e0, e0 + 1):
-                    i, a = divmod(e * C, GATHER)
                     mx(
                         bank[:, (e - e0) * C : (e - e0 + 1) * C],
                         w_codes[h],
                         w_scales[h],
                         e,
-                        slot_words[i][:, a : a + C],
-                        slot_scales[i][:, a : a + C],
+                        slot_words[e],
+                        slot_scales[e],
                     )
                 nc.scalar.copy(y[h][:, e0 * C : (e0 + 2) * C], bank[:])
 
-        quantize_experts(0, 0, 4)
-        quantize_experts(0, 4, 4)
+        quantize_experts(0, 0)
         multiply_experts(0, 0, 8)
-        slot_scales.append(on_bytes_of_w(10, [P, GATHER], U8, "slot_scales3")[:])
-        gather_scales(3)
-        quantize_experts(0, 8, 4)
-        multiply_experts(0, 8, 4)
-        last_scales = on_bytes_of_w(11, [P, SLOTS - 4 * GATHER], U8, "slot_scales4")
-        slot_scales.extend([last_scales[:, :GATHER], last_scales[:, GATHER:]])
-        gather_scales(4)
-        gather_scales(5)
-        quantize_experts(0, 12, 2)
-        quantize_experts(0, 14, 2)
-        multiply_experts(0, 12, 4)
+        gather_words(on_bytes_of_w(6, [P, 4 * C], U32, "slot_words12"), 12)
+        gather_scales(on_bytes_of_w(8, [P, 6 * C], U8, "slot_scales8"), 8)
+        quantize_experts(0, 8)
+        gather_scales(on_bytes_of_w(15, [P, 2 * C], U8, "slot_scales14"), 14)
+        multiply_experts(0, 8, 8)
 
-        ws_bf = keep.tile([P, 2, P, PACK], BF16, name="ws_bf", align_bytes=64)
+        w_codes.append(shared.tile([P, E * P], U32, name="w_codes1", tag="late", align_bytes=64))
+        ws_bf = shared.tile([P, 2, P, PACK], BF16, name="ws_bf", tag="codes0", align_bytes=64)
         ws_codes = keep.tile([P, N], U32, name="ws_codes", align_bytes=64)
         ws_scales = keep.tile([P, N], U8, name="ws_scales", align_bytes=64)
+        for e in (E - 2, E - 1):
+            interleave(w_bf[1, 8][:, e % 8, :, :], e, 1)
         interleave_both(ws_bf[:], E)
-        for e in range(early, E):
-            interleave(w_bf[:, 1, e, :, :], e, 1)
-        for first in range(0, E, 4):
-            quantize_experts(1, first, 4)
+        quantize_experts(1, 0)
+        quantize_experts(1, 8)
         quantize(ws_codes[:], ws_scales[:], ws_bf[:])
 
         def multiply_shared(h):
             for t0 in range(0, T, BANK):
-                bank = psum.tile([P, BANK], F32, name="y_bank", tag="y_bank", bufs=3)
+                bank = psum.tile([P, BANK], F32, name="y_bank", tag="bank", bufs=4)
                 mx(bank[:], ws_codes, ws_scales, h, tok_words[:, t0 : t0 + BANK], tok_scales[:, t0 : t0 + BANK])
                 nc.scalar.copy(ys[h][:, t0 : t0 + BANK], bank[:])
 
-        multiply_experts(1, 0, early)
+        multiply_experts(1, 0, 8)
         multiply_shared(0)
-        multiply_experts(1, early, E - early)
+        multiply_experts(1, 8, 8)
 
         def product(dst, h, r, t0):
             width = dst.shape[1]
@@ -205,24 +210,23 @@ def tile_moe_shr_lin_none_kernel(
             )
             return dst
 
-        def turn(terms, turned_sb):
-            width = turned_sb.shape[1]
-            blocks = width // P
-            turned = psum.tile([P, BANK], F32, name="turned", tag="turned", bufs=3)
-            for i, term in enumerate(terms):
-                for b in range(blocks):
-                    nc.tensor.matmul(
-                        turned[:, b * P : (b + 1) * P],
-                        term[:, b * P : (b + 1) * P],
-                        ident[:],
-                        start=(i == 0 and b == 0),
-                        stop=(i == len(terms) - 1 and b == blocks - 1),
-                        is_transpose=True,
-                    )
-            nc.scalar.copy(turned_sb, turned[:, :width])
+        def turn(banks, term, t0, start, stop):
+            for a in range(0, term.shape[1], P):
+                c, b = divmod(t0 + a, BANK)
+                nc.tensor.matmul(
+                    banks[c][:, b : b + P],
+                    term[:, a : a + P],
+                    ident[:],
+                    start=(start and b == 0),
+                    stop=(stop and b == BANK - P),
+                    is_transpose=True,
+                )
+
+        def sum_banks():
+            return [psum.tile([P, BANK], F32, name="turned", tag="turned", bufs=4) for c in range(T // BANK)]
 
         def turn_back(turned_sb):
-            back = psum.tile([P, BANK], F32, name="back", tag="back", bufs=2)
+            back = psum.tile([P, BANK], F32, name="back", tag="bank", bufs=4)
             for b in range(turned_sb.shape[1] // P):
                 nc.tensor.transpose(back[:, b * P : (b + 1) * P], turned_sb[:, b * P : (b + 1) * P], ident[:])
             return back
@@ -236,40 +240,46 @@ def tile_moe_shr_lin_none_kernel(
             nc.scalar.copy(res[:], back[:])
             store(res[:], h, t0)
 
-        def lane(i, name):
-            return shared.tile([P, BANK], F32, name=name, tag="lane%d" % i)[:]
+        def lane(i, width, name):
+            return shared.tile([P, width], F32, name=name, tag="lane%d" % i)[:]
 
-        sums = []
+        banks = sum_banks()
+        turn(banks, ys[0][:], 0, True, False)
+        turn(banks, product(on_bytes_of_w(9, [P, T], F32, "prod0_0")[:], 0, 0, 0), 0, False, False)
+        rest = on_bytes_of_w(E, [P, TOP - 1, T], F32, "prod0_rest")
+        for r in range(1, TOP):
+            turn(banks, product(rest[:, r - 1, :], 0, r, 0), 0, False, r == TOP - 1)
+        sums = [lane(c, BANK, "sum0_%d" % c) for c in range(2)]
         for c in range(2):
-            pairs = [on_bytes_of_w(4 + 2 * c + i, [P, 2, BANK], F32, "prod%d_%d" % (c, i)) for i in range(2)]
-            prods = [product(pairs[r // 2][:, r % 2, :], 0, r, c * BANK) for r in range(TOP)]
-            sums.append(lane(c, "sum0_%d" % c))
-            turn(prods + [ys[0][:, c * BANK : (c + 1) * BANK]], sums[c])
+            nc.scalar.copy(sums[c], banks[c][:])
         multiply_shared(1)
         for c in range(2):
             finish(sums[c], 0, c * BANK)
 
-        pair = on_bytes_of_w(8, [P, 2, BANK], F32, "prod2")
-        prods = [product(pair[:, r, :], 1, r, 0) for r in range(2)]
-        prods += [product(lane(r % 2, "prod2_%d" % r), 1, r, 0) for r in (2, 3)]
-        turned_sb = ring.tile([P, BANK], F32, name="turned_sb", tag="turned_sb", bufs=3)
-        turn(prods[:2] + [ys[1][:, :BANK]] + prods[2:], turned_sb[:])
-        finish(turned_sb[:], 1, 0)
-
-        half = BANK // 2
-        wide = [product(lane(r, "prod3_%d" % r), 1, r, BANK) for r in range(2)]
-        third = lane(0, "prod3_2")
+        banks = sum_banks()
+        pair = on_bytes_of_w(4, [P, 2, T], F32, "prod1_first")
+        turn(banks, product(pair[:, 0, :], 1, 0, 0), 0, True, False)
+        turn(banks, ys[1][:], 0, False, False)
+        turn(banks, product(pair[:, 1, :], 1, 1, 0), 0, False, False)
+        third = lane(0, T, "prod1_2")
         backs = []
-        for a in (0, half):
-            product(third[:, a : a + half], 1, 2, BANK + a)
-            terms = [ys[1][:, BANK + a : BANK + a + half]] + [g[:, a : a + half] for g in wide + [third]]
-            turned_sb = ring.tile([P, BANK], F32, name="turned_sb", tag="turned_sb", bufs=3)
-            turn(terms, turned_sb[:, :half])
-            backs.append(turn_back(turned_sb[:, :half]))
-        last = lane(1, "prod3_3")
-        for a in (0, half):
-            product(last[:, a : a + half], 1, 3, BANK + a)
-        for a, back in zip((0, half), backs):
+        for t0 in range(0, T, BANK):
+            turn(banks, product(third[:, t0 : t0 + BANK], 1, 2, t0), t0, False, True)
+            turned_sb = ring.tile([P, BANK], F32, name="turned_sb", tag="turned_sb", bufs=2)
+            nc.scalar.copy(turned_sb[:], banks[t0 // BANK][:])
+            backs.append(turn_back(turned_sb[:]))
+        last = lane(1, T, "prod1_3")
+
+        def add_last(t0, width):
             res = ring.tile([P, BANK], F32, name="res", tag="res", bufs=3)
-            nc.vector.tensor_tensor(res[:, :half], back[:, :half], last[:, a : a + half], ADD)
-            store(res[:, :half], 1, BANK + a)
+            a = t0 % BANK
+            nc.vector.tensor_tensor(res[:, :width], backs[t0 // BANK][:, a : a + width], last[:, t0 : t0 + width], ADD)
+            store(res[:, :width], 1, t0)
+
+        pieces = ((0, 512), (512, 256), (768, 256))
+        product(last[:, :512], 1, 3, 0)
+        product(last[:, 512:768], 1, 3, 512)
+        add_last(*pieces[0])
+        product(last[:, 768:], 1, 3, 768)
+        add_last(*pieces[1])
+        add_last(*pieces[2])

@@ -59,14 +59,13 @@ def tile_moe_shr_lin_none_kernel(
 
         def load_w(e):
             rows = w[e].rearrange("(p j) n -> p j n", j=PACK)
-            if e != E - 1:
-                raw = on_bytes_of_w(e, [P, PACK, N], F32, "w_raw%d" % e)
-                nc.sync.dma_start(raw[:], rows)
-                return [raw[:, :, :P], raw[:, :, P:], raw[:]]
-            halves = [on_bytes_of_w(e, [P, PACK, P], F32, "w_last0"), keep.tile([P, PACK, P], F32, name="w_last1")]
-            for h in range(2):
-                nc.sync.dma_start(halves[h][:], rows[:, :, h * P : (h + 1) * P])
-            return [half[:] for half in halves]
+            raw = on_bytes_of_w(e, [P, PACK, N], F32, "w_raw%d" % e)
+            nc.sync.dma_start(raw[:], rows)
+            return [raw[:, :, :P], raw[:, :, P:], raw[:]]
+
+        def load_w_half(raw, e, h):
+            nc.sync.dma_start(raw[:], w[e].rearrange("(p j) n -> p j n", j=PACK)[:, :, h * P : (h + 1) * P])
+            return raw[:]
 
         def load_gate(r, h, g):
             nc.sync.dma_start(g, gate[r, h * P : (h + 1) * P, :])
@@ -77,7 +76,11 @@ def tile_moe_shr_lin_none_kernel(
             nc.sync.dma_start(raw[:], w[e : e + 2].rearrange("e (p j) n -> p e j n", j=PACK))
             return [[raw[:, i, :, :P], raw[:, i, :, P:]] for i in range(2)]
 
-        w_raw = [one for e in range(0, 8, 2) for one in load_w_pair(e)] + [load_w(e) for e in range(8, E)]
+        w_raw = [one for e in range(0, 8, 2) for one in load_w_pair(e)] + [load_w(e) for e in range(8, E - 2)]
+        for e in (E - 2, E - 1):
+            w_raw.append([load_w_half(on_bytes_of_w(e, [P, PACK, P], F32, "w_raw%d_0" % e), e, 0)])
+        for e in (E - 2, E - 1):
+            w_raw[e].append(load_w_half(keep.tile([P, PACK, P], F32, name="w_raw%d_1" % e), e, 1))
         gates = {}
         for r, pos in enumerate((pos1, pos2, pos3, pos4)):
             nc.sync.dma_start(pos_sb[r][:], pos)
@@ -90,7 +93,7 @@ def tile_moe_shr_lin_none_kernel(
         def gather(by_expert, dst, window, first):
             count = dst.shape[1] // C
             cols = slice(first * C // PER_COL, (first + count) * C // PER_COL)
-            nc.vector.tensor_copy(dst[:], window.indirect(offs_sb[:, cols]))
+            nc.vector.tensor_copy(dst, window.indirect(offs_sb[:, cols]))
             for i in range(count):
                 by_expert[first + i] = dst[:, i * C : (i + 1) * C]
 
@@ -117,11 +120,11 @@ def tile_moe_shr_lin_none_kernel(
                 out=codes.bitcast(FP8X4), scales=scales, in_=rounded.rearrange("p s n j -> p (s n j)")
             )
 
-        def mx(dst, codes, scales, s, words, word_scales):
+        def mx(dst, codes, scales, words, word_scales):
             nc.tensor.matmul_mx(
                 out=dst,
-                lhsT=codes[:, s * P : (s + 1) * P].bitcast(FP8X4),
-                lhsT_scale=scales[:, s * P : (s + 1) * P],
+                lhsT=codes.bitcast(FP8X4),
+                lhsT_scale=scales,
                 rhs=words.bitcast(FP8X4),
                 rhs_scale=word_scales,
                 start=True,
@@ -129,33 +132,35 @@ def tile_moe_shr_lin_none_kernel(
             )
 
         for first in (0, 6):
-            gather_words(keep.tile([P, 6 * C], U32, name="slot_words%d" % first, align_bytes=64), first)
+            gather_words(keep.tile([P, 6 * C], U32, name="slot_words%d" % first, align_bytes=64)[:], first)
         for first, count in ((0, 6), (6, 2)):
-            gather_scales(keep.tile([P, count * C], U8, name="slot_scales%d" % first, align_bytes=64), first)
+            gather_scales(keep.tile([P, count * C], U8, name="slot_scales%d" % first, align_bytes=64)[:], first)
 
-        w_bf = {
-            (0, 0): keep.tile([P, 8, P, PACK], BF16, name="w_bf00", align_bytes=64),
-            (0, 8): shared.tile([P, 8, P, PACK], BF16, name="w_bf08", tag="late", align_bytes=64),
-            (1, 0): keep.tile([P, 8, P, PACK], BF16, name="w_bf10", align_bytes=64),
-            (1, 8): keep.tile([P, 8, P, PACK], BF16, name="w_bf18", align_bytes=64),
-        }
+        groups = ((0, 8), (8, 4), (12, 4))
+        w_bf = {}
+        rounded = {}
+        for h in range(2):
+            for first, count in groups:
+                w_bf[h, first] = keep.tile([P, count, P, PACK], BF16, name="w_bf%d_%d" % (h, first), align_bytes=64)
+                for i in range(count):
+                    rounded[h, first + i] = w_bf[h, first][:, i, :, :]
         for e in range(E):
-            interleave(w_bf[0, e // 8 * 8][:, e % 8, :, :], e, 0)
+            interleave(rounded[0, e], e, 0)
         for e in range(E - 2):
-            nc.gpsimd.tensor_scalar(
-                w_bf[1, e // 8 * 8][:, e % 8, :, :], w_raw[e][1].rearrange("p j n -> p n j"), 1.0, 0.0, MULT, ADD
-            )
+            nc.gpsimd.tensor_scalar(rounded[1, e], w_raw[e][1].rearrange("p j n -> p n j"), 1.0, 0.0, MULT, ADD)
         for r in range(0, TOP, 2):
             pair = on_bytes_of_w(r, [P, 2, T], F32, "gate%d_1" % r)
             for i in range(2):
                 gates[r + i, 1] = load_gate(r + i, 1, pair[:, i, :])
 
-        w_codes = [shared.tile([P, E * P], U32, name="w_codes0", tag="codes0", align_bytes=64)]
+        w_codes = {}
         w_scales = [keep.tile([P, E * P], U8, name="w_scales%d" % h, align_bytes=64) for h in range(2)]
 
-        def quantize_experts(h, first):
-            cols = slice(first * P, (first + 8) * P)
-            quantize(w_codes[h][:, cols], w_scales[h][:, cols], w_bf[h, first][:])
+        def quantize_experts(h, first, codes):
+            count = codes.shape[1] // P
+            quantize(codes, w_scales[h][:, first * P : (first + count) * P], w_bf[h, first][:])
+            for i in range(count):
+                w_codes[h, first + i] = codes[:, i * P : (i + 1) * P]
 
         def multiply_experts(h, first, count):
             for e0 in range(first, first + count, 2):
@@ -163,37 +168,41 @@ def tile_moe_shr_lin_none_kernel(
                 for e in (e0, e0 + 1):
                     mx(
                         bank[:, (e - e0) * C : (e - e0 + 1) * C],
-                        w_codes[h],
-                        w_scales[h],
-                        e,
+                        w_codes[h, e],
+                        w_scales[h][:, e * P : (e + 1) * P],
                         slot_words[e],
                         slot_scales[e],
                     )
                 nc.scalar.copy(y[h][:, e0 * C : (e0 + 2) * C], bank[:])
 
-        quantize_experts(0, 0)
+        quantize_experts(0, 0, keep.tile([P, 8 * P], U32, name="codes0_0", align_bytes=64)[:])
         multiply_experts(0, 0, 8)
-        gather_words(on_bytes_of_w(6, [P, 4 * C], U32, "slot_words12"), 12)
-        gather_scales(on_bytes_of_w(8, [P, 6 * C], U8, "slot_scales8"), 8)
-        quantize_experts(0, 8)
-        gather_scales(on_bytes_of_w(15, [P, 2 * C], U8, "slot_scales14"), 14)
+        gather_words(on_bytes_of_w(6, [P, 4 * C], U32, "slot_words12")[:], 12)
+        late_scales = on_bytes_of_w(8, [P, 8 * C], U8, "slot_scales8")
+        gather_scales(late_scales[:, : 6 * C], 8)
+        gather_scales(late_scales[:, 6 * C :], 14)
+        quantize_experts(1, 8, keep.tile([P, 4 * P], U32, name="codes1_8", align_bytes=64)[:])
+        quantize_experts(0, 8, on_bytes_of_w(14, [P, 4 * P], U32, "codes0_8")[:])
+        last_codes = shared.tile([P, 4 * P], U32, name="codes0_12", tag="last_codes", align_bytes=64)
+        quantize_experts(0, 12, last_codes[:])
         multiply_experts(0, 8, 8)
 
-        w_codes.append(shared.tile([P, E * P], U32, name="w_codes1", tag="late", align_bytes=64))
-        ws_bf = shared.tile([P, 2, P, PACK], BF16, name="ws_bf", tag="codes0", align_bytes=64)
+        ws_bf = shared.tile([P, 2, P, PACK], BF16, name="ws_bf", tag="last_codes", align_bytes=64)
         ws_codes = keep.tile([P, N], U32, name="ws_codes", align_bytes=64)
         ws_scales = keep.tile([P, N], U8, name="ws_scales", align_bytes=64)
         for e in (E - 2, E - 1):
-            interleave(w_bf[1, 8][:, e % 8, :, :], e, 1)
+            interleave(rounded[1, e], e, 1)
         interleave_both(ws_bf[:], E)
-        quantize_experts(1, 0)
-        quantize_experts(1, 8)
+        late_codes = on_bytes_of_w(15, [P, 12 * P], U32, "codes1_rest")
+        quantize_experts(1, 0, late_codes[:, : 8 * P])
+        quantize_experts(1, 12, late_codes[:, 8 * P :])
         quantize(ws_codes[:], ws_scales[:], ws_bf[:])
 
         def multiply_shared(h):
             for t0 in range(0, T, BANK):
                 bank = psum.tile([P, BANK], F32, name="y_bank", tag="bank", bufs=4)
-                mx(bank[:], ws_codes, ws_scales, h, tok_words[:, t0 : t0 + BANK], tok_scales[:, t0 : t0 + BANK])
+                cols = slice(h * P, (h + 1) * P)
+                mx(bank[:], ws_codes[:, cols], ws_scales[:, cols], tok_words[:, t0 : t0 + BANK], tok_scales[:, t0 : t0 + BANK])
                 nc.scalar.copy(ys[h][:, t0 : t0 + BANK], bank[:])
 
         multiply_experts(1, 0, 8)

@@ -139,15 +139,24 @@ def tile_moe_shr_lin_none_kernel(
         groups = ((0, 8), (8, 4), (12, 4))
         w_bf = {}
         rounded = {}
-        for h in range(2):
-            for first, count in groups:
-                w_bf[h, first] = keep.tile([P, count, P, PACK], BF16, name="w_bf%d_%d" % (h, first), align_bytes=64)
-                for i in range(count):
-                    rounded[h, first + i] = w_bf[h, first][:, i, :, :]
+
+        def rounded_tile(h, first, count, tag):
+            name = "w_bf%d_%d" % (h, first)
+            w_bf[h, first] = shared.tile([P, count, P, PACK], BF16, name=name, tag=tag or name, align_bytes=64)
+            for i in range(count):
+                rounded[h, first + i] = w_bf[h, first][:, i, :, :]
+
+        def interleave_on_gpsimd(e):
+            nc.gpsimd.tensor_scalar(rounded[1, e], w_raw[e][1].rearrange("p j n -> p n j"), 1.0, 0.0, MULT, ADD)
+
+        for first, count in groups:
+            rounded_tile(0, first, count, None)
+        rounded_tile(1, 0, 8, None)
+        rounded_tile(1, 12, 4, None)
         for e in range(E):
             interleave(rounded[0, e], e, 0)
-        for e in range(E - 2):
-            nc.gpsimd.tensor_scalar(rounded[1, e], w_raw[e][1].rearrange("p j n -> p n j"), 1.0, 0.0, MULT, ADD)
+        for e in range(8):
+            interleave_on_gpsimd(e)
         for r in range(0, TOP, 2):
             pair = on_bytes_of_w(r, [P, 2, T], F32, "gate%d_1" % r)
             for i in range(2):
@@ -177,12 +186,16 @@ def tile_moe_shr_lin_none_kernel(
 
         quantize_experts(0, 0, keep.tile([P, 8 * P], U32, name="codes0_0", align_bytes=64)[:])
         multiply_experts(0, 0, 8)
+        rounded_tile(1, 8, 4, "w_bf0_0")
+        for e in range(8, E - 2):
+            interleave_on_gpsimd(e)
         gather_words(on_bytes_of_w(6, [P, 4 * C], U32, "slot_words12")[:], 12)
         late_scales = on_bytes_of_w(8, [P, 8 * C], U8, "slot_scales8")
         gather_scales(late_scales[:, : 6 * C], 8)
         gather_scales(late_scales[:, 6 * C :], 14)
-        quantize_experts(1, 8, keep.tile([P, 4 * P], U32, name="codes1_8", align_bytes=64)[:])
-        quantize_experts(0, 8, on_bytes_of_w(14, [P, 4 * P], U32, "codes0_8")[:])
+        middle_codes = on_bytes_of_w(14, [P, 2, 4 * P], U32, "codes_8")
+        for h in range(2):
+            quantize_experts(h, 8, middle_codes[:, h, :])
         last_codes = shared.tile([P, 4 * P], U32, name="codes0_12", tag="last_codes", align_bytes=64)
         quantize_experts(0, 12, last_codes[:])
         multiply_experts(0, 8, 8)

from contextlib import ExitStack

import concourse.mybir as mybir
from concourse.masks import make_identity

K, T, E, C, N = 512, 1024, 16, 256, 256
TOP = 4
SLOTS = E * C
FLOPS = 2 * K * N * (SLOTS + T)

F32 = mybir.dt.float32
BF16 = mybir.dt.bfloat16
I32 = mybir.dt.int32
U32 = mybir.dt.uint32
U16 = mybir.dt.uint16
U8 = mybir.dt.uint8
FP8X4 = mybir.dt.float8_e4m3fn_x4
MULT = mybir.AluOpType.mult
ADD = mybir.AluOpType.add

P = 128
PACK = 4
BANK = 512
PER_COL = 16
GATHER = 1536
WINDOW = 2048


def tile_moe_shr_lin_none_kernel(
    tc, x_words, x_scales, w, gate, offs, pos1, pos2, pos3, pos4, out
):
    nc = tc.nc
    with ExitStack() as ctx:
        keep = ctx.enter_context(tc.tile_pool(name="keep", bufs=1))
        shared = ctx.enter_context(tc.tile_pool(name="shared", bufs=1))
        ring = ctx.enter_context(tc.tile_pool(name="ring", bufs=2))
        psum = ctx.enter_context(tc.psum_pool(name="psum", bufs=1))

        offs_sb = keep.tile([P, SLOTS // PER_COL], U16, name="offs_sb")
        pos_sb = [keep.tile([P, T // PER_COL], U16, name="pos_sb%d" % r) for r in range(TOP)]
        tok_words = keep.tile([P, WINDOW], I32, name="tok_words", align_bytes=64)
        tok_scales = keep.tile([P, WINDOW], U8, name="tok_scales", align_bytes=64)
        y = [keep.tile([P, SLOTS], F32, name="y%d" % h) for h in range(2)]
        ys = [keep.tile([P, T], F32, name="ys%d" % h) for h in range(2)]
        ident = keep.tile([P, P], F32, name="ident")

        nc.sync.dma_start(offs_sb[:], offs)
        nc.sync.dma_start(tok_words[:, :T], x_words[0].rearrange("p t r -> p (t r)").bitcast(I32))
        nc.gpsimd.memset(tok_scales[:].bitcast(I32), 0)
        nc.gpsimd.memset(tok_words[:, T:], 0)
        for q in range(4):
            nc.sync.dma_start(
                tok_scales[32 * q : 32 * q + 4, :T].bitcast(I32), x_scales[0, 4 * q : 4 * q + 4, :].bitcast(I32)
            )
        make_identity(nc, ident[:])

        def on_bytes_of_w(e, shape, dtype, name):
            return shared.tile(shape, dtype, name=name, tag="w%d" % e, align_bytes=64)

        def load_w(e):
            rows = w[e].rearrange("(p j) n -> p j n", j=PACK)
            raw = on_bytes_of_w(e, [P, PACK, N], F32, "w_raw%d" % e)
            nc.sync.dma_start(raw[:], rows)
            return [raw[:, :, :P], raw[:, :, P:], raw[:]]

        def load_w_half(raw, e, h):
            nc.sync.dma_start(raw[:], w[e].rearrange("(p j) n -> p j n", j=PACK)[:, :, h * P : (h + 1) * P])
            return raw[:]

        def load_gate(r, h, g):
            nc.sync.dma_start(g, gate[r, h * P : (h + 1) * P, :])
            return g

        def load_w_pair(e):
            raw = on_bytes_of_w(e, [P, 2, PACK, N], F32, "w_raw%d" % e)
            nc.sync.dma_start(raw[:], w[e : e + 2].rearrange("e (p j) n -> p e j n", j=PACK))
            return [[raw[:, i, :, :P], raw[:, i, :, P:]] for i in range(2)]

        w_raw = [one for e in range(0, 8, 2) for one in load_w_pair(e)] + [load_w(e) for e in range(8, E - 2)]
        for e in (E - 2, E - 1):
            w_raw.append([load_w_half(on_bytes_of_w(e, [P, PACK, P], F32, "w_raw%d_0" % e), e, 0)])
        for e in (E - 2, E - 1):
            w_raw[e].append(load_w_half(keep.tile([P, PACK, P], F32, name="w_raw%d_1" % e), e, 1))
        gates = {}
        for r, pos in enumerate((pos1, pos2, pos3, pos4)):
            nc.sync.dma_start(pos_sb[r][:], pos)
            gates[r, 0] = load_gate(r, 0, keep.tile([P, T], F32, name="gate%d_0" % r)[:])
            if r == 0:
                w_raw.append(load_w(E))

        slot_words, slot_scales = {}, {}

        def gather(by_expert, dst, window, first):
            count = dst.shape[1] // C
            cols = slice(first * C // PER_COL, (first + count) * C // PER_COL)
            nc.vector.tensor_copy(dst, window.indirect(offs_sb[:, cols]))
            for i in range(count):
                by_expert[first + i] = dst[:, i * C : (i + 1) * C]

        def gather_words(dst, first):
            gather(slot_words, dst, tok_words[:].bitcast(U32), first)

        def gather_scales(dst, first):
            gather(slot_scales, dst, tok_scales[:], first)

        def interleave(dst, e, h):
            nc.scalar.copy(
                dst.rearrange("p (c i) j -> p c j i", i=4),
                w_raw[e][h].rearrange("p j (c i) -> p c j i", i=4),
            )

        def interleave_both(dst, e):
            nc.scalar.copy(
                dst.rearrange("p h (c i) j -> p h c j i", i=4),
                w_raw[e][2].rearrange("p j (h c i) -> p h c j i", h=2, i=4),
            )

        def quantize(codes, scales, rounded):
            nc.vector.quantize_mx(
                out=codes.bitcast(FP8X4), scales=scales, in_=rounded.rearrange("p s n j -> p (s n j)")
            )

        def mx(dst, codes, scales, words, word_scales):
            nc.tensor.matmul_mx(
                out=dst,
                lhsT=codes.bitcast(FP8X4),
                lhsT_scale=scales,
                rhs=words.bitcast(FP8X4),
                rhs_scale=word_scales,
                start=True,
                stop=True,
            )

        for first in (0, 6):
            gather_words(keep.tile([P, 6 * C], U32, name="slot_words%d" % first, align_bytes=64)[:], first)
        for first, count in ((0, 6), (6, 2)):
            gather_scales(keep.tile([P, count * C], U8, name="slot_scales%d" % first, align_bytes=64)[:], first)

        groups = ((0, 8), (8, 4), (12, 4))
        w_bf = {}
        rounded = {}

        def rounded_tile(h, first, count, tag):
            name = "w_bf%d_%d" % (h, first)
            w_bf[h, first] = shared.tile([P, count, P, PACK], BF16, name=name, tag=tag or name, align_bytes=64)
            for i in range(count):
                rounded[h, first + i] = w_bf[h, first][:, i, :, :]

        def interleave_on_gpsimd(e):
            nc.gpsimd.tensor_scalar(rounded[1, e], w_raw[e][1].rearrange("p j n -> p n j"), 1.0, 0.0, MULT, ADD)

        for first, count in groups:
            rounded_tile(0, first, count, None)
        rounded_tile(1, 0, 8, None)
        rounded_tile(1, 12, 4, None)
        for e in range(E):
            interleave(rounded[0, e], e, 0)
        for e in range(8):
            interleave_on_gpsimd(e)
        for r in range(0, TOP, 2):
            pair = on_bytes_of_w(r, [P, 2, T], F32, "gate%d_1" % r)
            for i in range(2):
                gates[r + i, 1] = load_gate(r + i, 1, pair[:, i, :])

        w_codes = {}
        w_scales = [keep.tile([P, E * P], U8, name="w_scales%d" % h, align_bytes=64) for h in range(2)]

        def quantize_experts(h, first, codes):
            count = codes.shape[1] // P
            quantize(codes, w_scales[h][:, first * P : (first + count) * P], w_bf[h, first][:])
            for i in range(count):
                w_codes[h, first + i] = codes[:, i * P : (i + 1) * P]

        def multiply_experts(h, first, count):
            for e0 in range(first, first + count, 2):
                bank = psum.tile([P, BANK], F32, name="y_bank", tag="bank", bufs=4)
                for e in (e0, e0 + 1):
                    mx(
                        bank[:, (e - e0) * C : (e - e0 + 1) * C],
                        w_codes[h, e],
                        w_scales[h][:, e * P : (e + 1) * P],
                        slot_words[e],
                        slot_scales[e],
                    )
                nc.scalar.copy(y[h][:, e0 * C : (e0 + 2) * C], bank[:])

        quantize_experts(0, 0, keep.tile([P, 8 * P], U32, name="codes0_0", align_bytes=64)[:])
        multiply_experts(0, 0, 8)
        rounded_tile(1, 8, 4, "w_bf0_0")
        for e in range(8, E - 2):
            interleave_on_gpsimd(e)
        gather_words(on_bytes_of_w(6, [P, 4 * C], U32, "slot_words12")[:], 12)
        late_scales = on_bytes_of_w(8, [P, 8 * C], U8, "slot_scales8")
        gather_scales(late_scales[:, : 6 * C], 8)
        gather_scales(late_scales[:, 6 * C :], 14)
        middle_codes = on_bytes_of_w(14, [P, 2, 4 * P], U32, "codes_8")
        for h in range(2):
            quantize_experts(h, 8, middle_codes[:, h, :])
        last_codes = shared.tile([P, 4 * P], U32, name="codes0_12", tag="last_codes", align_bytes=64)
        quantize_experts(0, 12, last_codes[:])
        multiply_experts(0, 8, 8)

        ws_bf = shared.tile([P, 2, P, PACK], BF16, name="ws_bf", tag="last_codes", align_bytes=64)
        ws_codes = keep.tile([P, N], U32, name="ws_codes", align_bytes=64)
        ws_scales = keep.tile([P, N], U8, name="ws_scales", align_bytes=64)
        for e in (E - 2, E - 1):
            interleave(rounded[1, e], e, 1)
        interleave_both(ws_bf[:], E)
        late_codes = on_bytes_of_w(15, [P, 12 * P], U32, "codes1_rest")
        quantize_experts(1, 0, late_codes[:, : 8 * P])
        quantize_experts(1, 12, late_codes[:, 8 * P :])
        quantize(ws_codes[:], ws_scales[:], ws_bf[:])

        def multiply_shared(h):
            for t0 in range(0, T, BANK):
                bank = psum.tile([P, BANK], F32, name="y_bank", tag="bank", bufs=4)
                cols = slice(h * P, (h + 1) * P)
                mx(bank[:], ws_codes[:, cols], ws_scales[:, cols], tok_words[:, t0 : t0 + BANK], tok_scales[:, t0 : t0 + BANK])
                nc.scalar.copy(ys[h][:, t0 : t0 + BANK], bank[:])

        multiply_experts(1, 0, 8)
        multiply_shared(0)
        multiply_experts(1, 8, 8)

        def product(dst, h, r, t0):
            width = dst.shape[1]
            nc.vector.tensor_tensor(
                dst,
                y[h][:].indirect(pos_sb[r][:, t0 // PER_COL : (t0 + width) // PER_COL]),
                gates[r, h][:, t0 : t0 + width],
                MULT,
            )
            return dst

        def turn(banks, term, t0, start, stop):
            for a in range(0, term.shape[1], P):
                c, b = divmod(t0 + a, BANK)
                nc.tensor.matmul(
                    banks[c][:, b : b + P],
                    term[:, a : a + P],
                    ident[:],
                    start=(start and b == 0),
                    stop=(stop and b == BANK - P),
                    is_transpose=True,
                )

        def sum_banks():
            return [psum.tile([P, BANK], F32, name="turned", tag="turned", bufs=4) for c in range(T // BANK)]

        def turn_back(turned_sb):
            back = psum.tile([P, BANK], F32, name="back", tag="bank", bufs=4)
            for b in range(turned_sb.shape[1] // P):
                nc.tensor.transpose(back[:, b * P : (b + 1) * P], turned_sb[:, b * P : (b + 1) * P], ident[:])
            return back

        def store(res, h, t0):
            nc.sync.dma_start(out[h * P : (h + 1) * P, t0 : t0 + res.shape[1]], res)

        def finish(turned_sb, h, t0):
            back = turn_back(turned_sb)
            res = ring.tile([P, BANK], F32, name="res", tag="res", bufs=3)
            nc.scalar.copy(res[:], back[:])
            store(res[:], h, t0)

        def lane(i, width, name):
            return shared.tile([P, width], F32, name=name, tag="lane%d" % i)[:]

        banks = sum_banks()
        turn(banks, ys[0][:], 0, True, False)
        turn(banks, product(on_bytes_of_w(9, [P, T], F32, "prod0_0")[:], 0, 0, 0), 0, False, False)
        rest = on_bytes_of_w(E, [P, TOP - 1, T], F32, "prod0_rest")
        for r in range(1, TOP):
            turn(banks, product(rest[:, r - 1, :], 0, r, 0), 0, False, r == TOP - 1)
        sums = [lane(c, BANK, "sum0_%d" % c) for c in range(2)]
        for c in range(2):
            nc.scalar.copy(sums[c], banks[c][:])
        multiply_shared(1)
        for c in range(2):
            finish(sums[c], 0, c * BANK)

        banks = sum_banks()
        pair = on_bytes_of_w(4, [P, 2, T], F32, "prod1_first")
        turn(banks, product(pair[:, 0, :], 1, 0, 0), 0, True, False)
        turn(banks, ys[1][:], 0, False, False)
        turn(banks, product(pair[:, 1, :], 1, 1, 0), 0, False, False)
        third = lane(0, T, "prod1_2")
        backs = []
        for t0 in range(0, T, BANK):
            turn(banks, product(third[:, t0 : t0 + BANK], 1, 2, t0), t0, False, True)
            turned_sb = ring.tile([P, BANK], F32, name="turned_sb", tag="turned_sb", bufs=2)
            nc.scalar.copy(turned_sb[:], banks[t0 // BANK][:])
            backs.append(turn_back(turned_sb[:]))
        last = lane(1, T, "prod1_3")

        def add_last(t0, width):
            res = ring.tile([P, BANK], F32, name="res", tag="res", bufs=3)
            a = t0 % BANK
            nc.vector.tensor_tensor(res[:, :width], backs[t0 // BANK][:, a : a + width], last[:, t0 : t0 + width], ADD)
            store(res[:, :width], 1, t0)

        pieces = ((0, 512), (512, 256), (768, 256))
        product(last[:, :512], 1, 3, 0)
        product(last[:, 512:768], 1, 3, 512)
        add_last(*pieces[0])
        product(last[:, 768:], 1, 3, 768)
        add_last(*pieces[1])
        add_last(*pieces[2])
